import numpy as np
import ml_dtypes


def mxq(x, axis, fmt="e4m3"):
    dtype, down = {"e4m3": (ml_dtypes.float8_e4m3fn, 7), "e5m2": (ml_dtypes.float8_e5m2, 14)}[fmt]
    v = np.moveaxis(np.asarray(x, np.float32).astype(ml_dtypes.bfloat16).astype(np.float64), axis, -1)
    blocks = v.reshape(v.shape[:-1] + (-1, 32))
    amax = np.abs(blocks).max(-1, keepdims=True)
    byte = np.maximum(np.where(amax > 0, np.frexp(amax)[1] - 1 + 127, 0) - down, 1)
    scale = np.exp2(byte - 127.0)
    codes = (blocks / scale).astype(np.float32).astype(dtype).astype(np.float64)
    return np.moveaxis((codes * scale).reshape(v.shape), -1, axis)


WIDE = False


def mx_kscale(k):
    if not WIDE:
        return np.ones(k)
    levels = np.array([10, -10, 5, -5, 0])
    if k % 512:
        return np.exp2(np.random.permutation(np.resize(levels, k // 32))).repeat(32)
    a = np.empty((k // 512, 16))
    for p in range(k // 512):
        a[p, :8] = np.random.permutation(np.resize(levels, 8))
        for g in range(8):
            far = levels[np.abs(levels - a[p, g]) >= 10]
            a[p, g + 8] = far[np.random.randint(len(far))]
    return np.exp2(a.ravel()).repeat(32)


def f64(x):
    return np.asarray(x).astype(np.float64)


def striped(idx):
    return np.tile(idx.reshape(-1, 16).T, (8, 1)).astype(np.uint16)


def unstriped(offs):
    return offs[:16].T.reshape(-1).astype(np.int64)


E2M1 = np.array([0.0, 0.5, 1.0, 1.5, 2.0, 3.0, 4.0, 6.0, -0.0, -0.5, -1.0, -1.5, -2.0, -3.0, -4.0, -6.0])


def pack_weight(w, fmt):
    k, n = w.shape
    w = f64(np.asarray(w, np.float32).astype(ml_dtypes.bfloat16)).reshape(k // 32, 32, n)
    amax = np.abs(w).max(1)
    if fmt == "e4m3":
        byte = np.frexp(amax)[1] - 1 + 127 - 7
    else:
        mant, ex = np.frexp(amax / 6.0)
        byte = np.where(mant > 0.5, ex, ex - 1) + 127
    byte = np.clip(np.where(amax > 0, byte, 1), 1, 254)
    scaled = (w * np.exp2(127.0 - byte)[:, None, :]).reshape(k, n).astype(np.float32)
    by_word = np.ascontiguousarray(scaled.reshape(k // 512, 128, 4, n).transpose(0, 1, 3, 2))
    if fmt == "e4m3":
        words = by_word.astype(ml_dtypes.float8_e4m3fn).view(np.uint8)
    else:
        c = by_word.astype(ml_dtypes.float4_e2m1fn).view(np.uint8) & 0xF
        words = (c[..., 0::2] | (c[..., 1::2] << 4)).reshape(k // 512, 128, 2 * n)
    return np.ascontiguousarray(words), np.ascontiguousarray(byte.astype(np.uint8).reshape(k // 512, 16, n))


def unpack_weight(words, scales, fmt):
    g, _, n = scales.shape
    words = np.ascontiguousarray(words).reshape(g, 128, n, -1)
    if fmt == "e4m3":
        vals = words.view(ml_dtypes.float8_e4m3fn).astype(np.float64)
    else:
        nib = np.empty((g, 128, n, 4), np.uint8)
        nib[..., 0::2] = words & 0xF
        nib[..., 1::2] = words >> 4
        vals = E2M1[nib]
    vals = vals * np.repeat(np.exp2(scales.astype(np.float64) - 127.0), 8, axis=1)[..., None]
    return vals.transpose(0, 1, 3, 2).reshape(g * 512, n)


def gelu(v):
    return 0.5 * v * (1.0 + np.tanh(np.sqrt(2.0 / np.pi) * (v + 0.044715 * v**3)))


K, H, T, S, P = 1536, 1024, 4096, 1024, 512

def setup_inputs():
    n = np.random.standard_normal
    s = mx_kscale(K)[:, None]
    u = mx_kscale(H)[:, None]
    tab_words, tab_scales = pack_weight(n((K, T)) * s, "e4m3")
    w2_words, w2_scales = pack_weight(1.5 * n((H, H)) / np.sqrt(H) / u, "e2m1")
    return {
        "tab_words": tab_words, "tab_scales": tab_scales,
        "offs": striped(np.random.permutation(T)[:S]),
        "pos1": striped(np.random.permutation(S)[:P]),
        "pos2": striped(np.random.permutation(S)[:P]),
        "w1": (n((K, H)) / np.sqrt(K) / s).astype(np.float32),
        "b1": (0.4 * n(H)).astype(np.float32),
        "gain": (np.exp(0.3 * n(H)) * u[:, 0]).astype(np.float32),
        "w2_words": w2_words, "w2_scales": w2_scales,
    }

def reference(tab_words, tab_scales, offs, pos1, pos2, w1, b1, gain, w2_words, w2_scales):
    v = unpack_weight(tab_words, tab_scales, "e4m3")[:, unstriped(offs)]
    W1 = mxq(f64(w1), 0, "e4m3")
    W2 = unpack_weight(w2_words, w2_scales, "e2m1")
    h = (W1.T @ v) + f64(b1)[:, None]
    old = h[:, unstriped(pos1)]
    x = old / (1.0 + np.exp(-old)) * f64(gain)[:, None]
    y = W2.T @ mxq(x, 0, "e4m3")
    t = y * h[:, unstriped(pos2)]
    lik = 1.0 / (1.0 + np.exp(-t))
    return np.log(lik)

@@ -1,0 +1,293 @@
+from contextlib import ExitStack
+
+import concourse.mybir as mybir
+
+K, H, T, S, NP = 1536, 1024, 4096, 1024, 512
+FLOPS = 2 * K * H * S + 2 * H * H * NP
+
+F32 = mybir.dt.float32
+BF16 = mybir.dt.bfloat16
+I32 = mybir.dt.int32
+U32 = mybir.dt.uint32
+U16 = mybir.dt.uint16
+U8 = mybir.dt.uint8
+FP8X4 = mybir.dt.float8_e4m3fn_x4
+FP4X4 = mybir.dt.float4_e2m1fn_x4
+ACT = mybir.ActivationFunctionType
+ALU = mybir.AluOpType
+
+P = 128
+PACK = 4
+PASS = P * PACK
+BANK = 512
+KP = K // PASS
+HP = H // PASS
+FLOOR = 2.0**-60
+CASTS = {
+    (1, 0): (("v", 0, 128),),
+    (1, 1): (("s", 0, 32), ("s", 32, 64), ("s", 64, 96), ("s", 96, 128),),
+    (1, 2): (("v", 0, 64),("s", 64, 96), ("s", 96, 128),),
+    (0, 0): (("s", 0, 128),),
+    (0, 1): (("v", 0, 128),),
+    (0, 2): (("s", 0, 64), ("v", 64, 108), ("s", 108, 128)),
+}
+GORDER = ((0, 1, 2), (0, 1, 2))
+CUTS = (((0, 256), (256, 512)), ((0, 256), (256, 384), (384, 512)))
+LOGIT_TAG = ("big2", "raw10")
+FUSED = ()
+GAIN_S = ()
+WEAVE = (("s", 0, 32), ("s", 32, 64), ("s", 64, 96), ("s", 96, 128))
+SKIP_TAG = ("raw11", "raw12", (1, 2), "xb1")
+GAIN_G = ()
+GROUPS = ((0, 4), (4, 8))
+
+
+def tile_list_gazette_pair_loglik_kernel(
+    tc, tab_words, tab_scales, offs, pos1, pos2, w1, b1, gain, w2_words, w2_scales, out
+):
+    nc = tc.nc
+    with ExitStack() as ctx:
+        lists = ctx.enter_context(tc.tile_pool(name="lists", bufs=1))
+        keep = ctx.enter_context(tc.tile_pool(name="keep", bufs=1))
+        psum = ctx.enter_context(tc.psum_pool(name="psum", bufs=8))
+
+        offs_sb = lists.tile([P, S // 16], U16, name="offs_sb")
+        pos1_sb = lists.tile([P, NP // 16], U16, name="pos1_sb")
+        pos2_sb = lists.tile([P, NP // 16], U16, name="pos2_sb")
+
+        tab_sc = keep.tile([P, T], U8, name="tab_sc", align_bytes=64)
+        nc.vector.memset(tab_sc[:].bitcast(I32), 0)
+        w2s_raw = keep.tile([P, HP * H], U8, name="w2s_raw", align_bytes=64)
+        nc.vector.memset(w2s_raw[:].bitcast(I32), 0)
+        floor = keep.tile([P, 1], F32, name="floor")
+        nc.vector.memset(floor[:], FLOOR)
+        warm = keep.tile([P, 1], F32, name="warm")
+        nc.scalar.activation(warm[:], floor[:], ACT.Silu)
+
+        tab = [keep.tile([P, T], I32, name=f"tab{g}", tag=f"big{g}", align_bytes=64) for g in range(KP)]
+        w1_raw = {}
+
+        def load_tab(g):
+            nc.sync.dma_start(tab[g][:], tab_words[g].rearrange("p n i -> p (n i)").bitcast(I32))
+
+        def load_w1(a, g, parts=1):
+            raw = keep.tile([P, PACK, PASS], F32, name=f"w1raw{a}{g}", tag=f"raw{a}{g}", align_bytes=64)
+            src = w1[g * PASS : (g + 1) * PASS, a * PASS : (a + 1) * PASS].rearrange("(p j) c -> p j c", j=PACK)
+            width = PASS // parts
+            for c0 in range(0, PASS, width):
+                nc.sync.dma_start(raw[:, :, c0 : c0 + width], src[:, :, c0 : c0 + width])
+            w1_raw[a, g] = raw
+
+        load_tab(0)
+        nc.sync.dma_start(offs_sb[:], offs)
+        for q in range(4):
+            nc.gpsimd.dma_start(
+                tab_sc[32 * q : 32 * q + 4 * KP, :].bitcast(I32),
+                tab_scales[:, 4 * q : 4 * q + 4, :].bitcast(I32),
+            )
+        w2w_raw = keep.tile([P, HP, H // 2], I32, name="w2w_raw", align_bytes=64)
+        nc.sync.dma_start(w2w_raw[:], w2_words.bitcast(I32).rearrange("a p w -> p a w"))
+        nc.sync.dma_start(pos1_sb[:], pos1)
+        nc.sync.dma_start(pos2_sb[:], pos2)
+        b1_sb = keep.tile([P, HP, PACK], F32, name="b1_sb")
+        nc.sync.dma_start(b1_sb[:], b1.rearrange("(a p t) -> p a t", a=HP, t=PACK))
+        gain_sb = keep.tile([P, HP, PACK], F32, name="gain_sb")
+        nc.sync.dma_start(gain_sb[:], gain.rearrange("(a p t) -> p a t", a=HP, t=PACK))
+        load_tab(1)
+        for q in range(4):
+            nc.sync.dma_start(
+                w2s_raw[32 * q : 32 * q + 4, :].bitcast(I32).rearrange("r (a w) -> r a w", a=HP),
+                w2_scales[:, 4 * q : 4 * q + 4, :].bitcast(I32).rearrange("a r w -> r a w"),
+            )
+        load_w1(0, 0)
+        load_tab(2)
+        load_w1(0, 1)
+        load_w1(0, 2, parts=2)
+        for g in range(KP):
+            load_w1(1, g)
+
+        v_words = [keep.tile([P, S], U32, name=f"vw{g}", align_bytes=64) for g in range(KP)]
+        v_sc = keep.tile([P, S], U8, name="v_sc", align_bytes=64)
+
+        def gather_words(g):
+            nc.vector.tensor_copy(v_words[g][:], tab[g][:].bitcast(U32).indirect(offs_sb[:]))
+
+        w1_codes, w1_sc = {}, {}
+
+        def quantise_w1(a, g, parts=1):
+            grouped = keep.tile([P, PASS * PACK], BF16, name=f"grp{a}{g}", tag=f"grp{g}", align_bytes=64)
+            dst = grouped[:].rearrange("p (t m j) -> p m t j", t=PACK, j=PACK)
+            src = w1_raw[a, g][:].rearrange("p j (m t) -> p m t j", t=PACK)
+            for eng, m0, m1 in CASTS[a, g]:
+                if eng == "v":
+                    nc.vector.tensor_copy(dst[:, m0:m1], src[:, m0:m1])
+                elif eng == "s":
+                    nc.scalar.copy(dst[:, m0:m1], src[:, m0:m1])
+                else:
+                    nc.gpsimd.tensor_scalar(dst[:, m0:m1], src[:, m0:m1], 1.0, 0.0, ALU.mult, ALU.add)
+            codes = keep.tile([P, PASS], U32, name=f"w1c{a}{g}", align_bytes=64)
+            scales = keep.tile([P, PASS], U8, name=f"w1s{a}{g}", align_bytes=64)
+            width = PASS // parts
+            for c0 in range(0, PASS, width):
+                nc.vector.quantize_mx(
+                    out=codes[:, c0 : c0 + width].bitcast(FP8X4),
+                    scales=scales[:, c0 : c0 + width],
+                    in_=grouped[:, PACK * c0 : PACK * (c0 + width)],
+                )
+            w1_codes[a, g], w1_sc[a, g] = codes, scales
+
+        h_acc = {}
+
+        def first_product(a, i, t):
+            g = GORDER[a][i]
+            for nh in range(S // BANK):
+                if i == 0:
+                    h_acc[a, t, nh] = psum.tile([P, BANK], F32, name=f"hacc{a}{t}{nh}", tag="acc")
+                nc.tensor.matmul_mx(
+                    out=h_acc[a, t, nh][:],
+                    lhsT=w1_codes[a, g][:, t * P : (t + 1) * P].bitcast(FP8X4),
+                    lhsT_scale=w1_sc[a, g][:, t * P : (t + 1) * P],
+                    rhs=v_words[g][:, nh * BANK : (nh + 1) * BANK].bitcast(FP8X4),
+                    rhs_scale=v_sc[4 * g :, nh * BANK : (nh + 1) * BANK],
+                    start=(i == 0),
+                    stop=(i == KP - 1),
+                )
+
+        h = {}
+
+        def leave_psum(a, t):
+            h[a, t] = keep.tile([P, S], F32, name=f"h{a}{t}")
+            for nh in range(S // BANK):
+                dst = h[a, t][:, nh * BANK : (nh + 1) * BANK]
+                if (a, t, nh) == (0, 0, 1):
+                    nc.vector.tensor_scalar(dst, h_acc[a, t, nh][:], b1_sb[:, a, t : t + 1], None, ALU.add)
+                else:
+                    nc.scalar.activation(dst, h_acc[a, t, nh][:], ACT.Identity, bias=b1_sb[:, a, t : t + 1])
+
+        old = {}
+
+        def pick_old(a, t):
+            if t == 0:
+                old[a] = keep.tile([P, PACK, NP], F32, name=f"old{a}", tag=f"pick{a}", align_bytes=64)
+            nc.vector.tensor_copy(old[a][:, t, :], h[a, t][:].indirect(pos1_sb[:]))
+
+        act = {}
+
+        def silu_old(a, t):
+            if t == 0:
+                act[a] = keep.tile([P, PACK, NP], F32, name=f"act{a}", tag=f"raw0{a}", align_bytes=64)
+            nc.scalar.activation(act[a][:, t, :], old[a][:, t, :], ACT.Silu)
+
+        x_codes, x_sc = {}, {}
+
+        def make_x(a):
+            xb = keep.tile([P, NP * PACK], BF16, name=f"xb{a}", tag=f"xb{a}", align_bytes=64)
+            if a in GAIN_S:
+                xp = keep.tile([P, PACK, NP], BF16, name=f"xp{a}", tag="grp0", align_bytes=64)
+                for t in range(PACK):
+                    nc.scalar.activation(xp[:, t, :], act[a][:, t, :], ACT.Copy, scale=gain_sb[:, a, t : t + 1])
+                for eng, c0, c1 in WEAVE:
+                    dst = xb[:].rearrange("p (c i t) -> p c t i", i=4, t=PACK)[:, c0:c1]
+                    src = xp[:].rearrange("p t (c i) -> p c t i", i=4)[:, c0:c1]
+                    if eng == "s":
+                        nc.scalar.copy(dst, src)
+                    else:
+                        nc.vector.tensor_copy(dst, src)
+            else:
+                eng = nc.gpsimd if a in GAIN_G else nc.vector
+                eng.tensor_tensor(
+                    xb[:].rearrange("p (c i t) -> p c t i", i=2, t=PACK),
+                    act[a][:].rearrange("p t (c i) -> p c t i", i=2),
+                    gain_sb[:, a, :].unsqueeze(1).unsqueeze(3).to_broadcast([P, NP // 2, PACK, 2]),
+                    ALU.mult,
+                )
+            x_codes[a] = keep.tile([P, NP], U32, name=f"xc{a}", align_bytes=64)
+            x_sc[a] = keep.tile([P, NP], U8, name=f"xs{a}", align_bytes=64)
+            nc.vector.quantize_mx(out=x_codes[a][:].bitcast(FP8X4), scales=x_sc[a][:], in_=xb[:])
+
+        gather_words(0)
+        nc.vector.tensor_copy(v_sc[:], tab_sc[:].indirect(offs_sb[:]))
+        gather_words(1)
+        gather_words(2)
+        quantise_w1(0, 0)
+        for t in range(PACK):
+            first_product(0, 0, t)
+        quantise_w1(0, 1)
+        quantise_w1(0, 2, parts=2)
+        for t in range(PACK):
+            first_product(0, 1, t)
+            first_product(0, 2, t)
+            leave_psum(0, t)
+
+        w2w = keep.tile([P, HP * H], U16, name="w2w", align_bytes=64)
+        nc.vector.tensor_copy(
+            w2w[:].rearrange("p (ab t m) -> p ab t m", t=PACK, m=P),
+            w2w_raw[:].rearrange("p a w -> p (a w)").bitcast(U16).rearrange("p (ab m t) -> p ab t m", t=PACK, m=P),
+        )
+        w2s = keep.tile([P, HP * H], U8, name="w2s", align_bytes=64)
+        nc.vector.tensor_copy(
+            w2s[:].rearrange("p (ab t m) -> p ab t m", t=PACK, m=P),
+            w2s_raw[:].rearrange("p (ab m t) -> p ab t m", t=PACK, m=P),
+        )
+
+        for t in range(PACK):
+            pick_old(0, t)
+        for g in range(KP):
+            quantise_w1(1, g)
+        for i in range(KP - 1):
+            for t in range(PACK):
+                first_product(1, i, t)
+        for t in range(PACK):
+            first_product(1, KP - 1, t)
+            leave_psum(1, t)
+        for t in range(PACK):
+            silu_old(0, t)
+        for t in range(PACK):
+            pick_old(1, t)
+            silu_old(1, t)
+        make_x(0)
+        make_x(1)
+        warm2 = keep.tile([P, 1], F32, name="warm2")
+        nc.scalar.activation(warm2[:], act[1][:, PACK - 1, 0:1], ACT.Sigmoid)
+
+        w2w8 = w2w[:].bitcast(U8)
+        skip = []
+        for t, tag in enumerate(SKIP_TAG):
+            if isinstance(tag, str):
+                room = keep.tile([P, NP], F32, name=f"skip{t}", tag=tag, align_bytes=64)
+                skip.append(room[:])
+            else:
+                skip.append(old[tag[0]][:, tag[1], :])
+        for gi, (u0, u1) in enumerate(GROUPS):
+            n = u1 - u0
+            logit = keep.tile([P, n, NP], F32, name=f"logit{gi}", tag=LOGIT_TAG[gi], align_bytes=64)
+            lik = keep.tile([P, n, NP], F32, name=f"lik{gi}", tag=f"big{gi}", align_bytes=64)
+            for b, t in (divmod(bt, PACK) for bt in range(u0, u1)):
+                y = psum.tile([P, BANK], F32, name=f"y{b}{t}", tag="acc")
+                for a in range(HP):
+                    c0 = a * H + b * PASS + t * P
+                    nc.tensor.matmul_mx(
+                        out=y[:],
+                        lhsT=w2w8[:, 2 * c0 : 2 * (c0 + P)].bitcast(FP4X4),
+                        lhsT_scale=w2s[:, c0 : c0 + P],
+                        rhs=x_codes[a][:].bitcast(FP8X4),
+                        rhs_scale=x_sc[a][:],
+                        start=(a == 0),
+                        stop=(a == HP - 1),
+                    )
+                u = PACK * b + t - u0
+                if (b, t) in FUSED:
+                    nc.scalar.copy(lik[:, u, :], y[:])
+                    nc.vector.tensor_tensor(logit[:, u, :], h[b, t][:].indirect(pos2_sb[:]), lik[:, u, :], ALU.mult)
+                else:
+                    nc.vector.tensor_copy(skip[t], h[b, t][:].indirect(pos2_sb[:]))
+                    nc.vector.tensor_tensor(logit[:, u, :], y[:], skip[t], ALU.mult)
+                nc.scalar.activation(lik[:, u, :], logit[:, u, :], ACT.Sigmoid)
+            for c0, c1 in CUTS[gi]:
+                nc.scalar.activation(lik[:, :, c0:c1], lik[:, :, c0:c1], ACT.Ln, bias=floor[:])
+                nc.vector.tensor_tensor(lik[:, :, c0:c1], lik[:, :, c0:c1], logit[:, :, c0:c1], ALU.min)
+                for b in range(HP):
+                    lo, hi = max(u0, PACK * b), min(u1, PACK * (b + 1))
+                    if lo < hi:
+                        rows = out[b * PASS : (b + 1) * PASS, :].rearrange("(p t) m -> p t m", t=PACK)
+                        nc.sync.dma_start(rows[:, lo - PACK * b : hi - PACK * b, c0:c1], lik[:, lo - u0 : hi - u0, c0:c1])

@@ -32,9 +32,11 @@ CASTS = {
     (0, 2): (("s", 0, 64), ("v", 64, 108), ("s", 108, 128)),
 }
 GORDER = ((0, 1, 2), (0, 1, 2))
-CUTS = (((0, 256), (256, 512)), ((0, 256), (256, 384), (384, 512)))
+CUTS = (((0, 4, 0, 256), (0, 4, 256, 512)), ((4, 5, 0, 512), (5, 6, 0, 512), (6, 7, 0, 512), (7, 8, 0, 512),))
 LOGIT_TAG = ("big2", "raw10")
 FUSED = ()
+SILU_WEAVE = ()
+HOLD = ("none", "last")
 GAIN_S = ()
 WEAVE = (("s", 0, 32), ("s", 32, 64), ("s", 64, 96), ("s", 96, 128))
 SKIP_TAG = ("raw11", "raw12", (1, 2), "xb1")
@@ -90,9 +92,9 @@ def tile_list_gazette_pair_loglik_kernel(
         nc.sync.dma_start(pos1_sb[:], pos1)
         nc.sync.dma_start(pos2_sb[:], pos2)
         b1_sb = keep.tile([P, HP, PACK], F32, name="b1_sb")
-        nc.sync.dma_start(b1_sb[:], b1.rearrange("(a p t) -> p a t", a=HP, t=PACK))
+        nc.scalar.dma_start(b1_sb[:], b1.rearrange("(a p t) -> p a t", a=HP, t=PACK))
         gain_sb = keep.tile([P, HP, PACK], F32, name="gain_sb")
-        nc.sync.dma_start(gain_sb[:], gain.rearrange("(a p t) -> p a t", a=HP, t=PACK))
+        nc.scalar.dma_start(gain_sb[:], gain.rearrange("(a p t) -> p a t", a=HP, t=PACK))
         load_tab(1)
         for q in range(4):
             nc.sync.dma_start(
@@ -116,8 +118,8 @@ def tile_list_gazette_pair_loglik_kernel(
 
         def quantise_w1(a, g, parts=1):
             grouped = keep.tile([P, PASS * PACK], BF16, name=f"grp{a}{g}", tag=f"grp{g}", align_bytes=64)
-            dst = grouped[:].rearrange("p (t m j) -> p m t j", t=PACK, j=PACK)
-            src = w1_raw[a, g][:].rearrange("p j (m t) -> p m t j", t=PACK)
+            dst = grouped[:].rearrange("p (t m j) -> p m j t", t=PACK, j=PACK)
+            src = w1_raw[a, g][:].rearrange("p j (m t) -> p m j t", t=PACK)
             for eng, m0, m1 in CASTS[a, g]:
                 if eng == "v":
                     nc.vector.tensor_copy(dst[:, m0:m1], src[:, m0:m1])
@@ -176,7 +178,13 @@ def tile_list_gazette_pair_loglik_kernel(
         def silu_old(a, t):
             if t == 0:
                 act[a] = keep.tile([P, PACK, NP], F32, name=f"act{a}", tag=f"raw0{a}", align_bytes=64)
-            nc.scalar.activation(act[a][:, t, :], old[a][:, t, :], ACT.Silu)
+            if not SILU_WEAVE:
+                nc.scalar.activation(act[a][:, t, :], old[a][:, t, :], ACT.Silu)
+            elif t == PACK - 1:
+                dst = act[a][:].rearrange("p t m -> p (t m)").rearrange("p (c i t) -> p c t i", i=4, t=PACK)
+                src = old[a][:].rearrange("p t (c i) -> p c t i", i=4)
+                for c0, c1 in SILU_WEAVE:
+                    nc.scalar.activation(dst[:, c0:c1], src[:, c0:c1], ACT.Silu)
 
         x_codes, x_sc = {}, {}
 
@@ -193,6 +201,16 @@ def tile_list_gazette_pair_loglik_kernel(
                         nc.scalar.copy(dst, src)
                     else:
                         nc.vector.tensor_copy(dst, src)
+            elif SILU_WEAVE:
+                dst = xb[:].rearrange("p (m t) -> p m t", t=PACK)
+                src = act[a][:].rearrange("p t m -> p (t m)").rearrange("p (m t) -> p m t", t=PACK)
+                for c0, c1 in SILU_WEAVE:
+                    nc.vector.tensor_tensor(
+                        dst[:, 4 * c0 : 4 * c1],
+                        src[:, 4 * c0 : 4 * c1],
+                        gain_sb[:, a, :].unsqueeze(1).to_broadcast([P, 4 * (c1 - c0), PACK]),
+                        ALU.mult,
+                    )
             else:
                 eng = nc.gpsimd if a in GAIN_G else nc.vector
                 eng.tensor_tensor(
@@ -248,7 +266,7 @@ def tile_list_gazette_pair_loglik_kernel(
         make_x(0)
         make_x(1)
         warm2 = keep.tile([P, 1], F32, name="warm2")
-        nc.scalar.activation(warm2[:], act[1][:, PACK - 1, 0:1], ACT.Sigmoid)
+        nc.scalar.activation(warm2[:], act[1][:, PACK - 1, NP - 1 : NP], ACT.Sigmoid)
 
         w2w8 = w2w[:].bitcast(U8)
         skip = []
@@ -258,36 +276,45 @@ def tile_list_gazette_pair_loglik_kernel(
                 skip.append(room[:])
             else:
                 skip.append(old[tag[0]][:, tag[1], :])
+        logit = keep.tile([P, HP * PACK, NP], F32, name="logit", tag="big0", align_bytes=64)
+        lik = keep.tile([P, HP * PACK, NP], F32, name="lik", tag="big1", align_bytes=64)
+        ys, y_sb = {}, {}
+        for u in range(HP * PACK):
+            b, t = divmod(u, PACK)
+            ys[u] = psum.tile([P, BANK], F32, name=f"y{u}", tag="acc")
+            for a in range(HP):
+                c0 = a * H + b * PASS + t * P
+                nc.tensor.matmul_mx(
+                    out=ys[u][:],
+                    lhsT=w2w8[:, 2 * c0 : 2 * (c0 + P)].bitcast(FP4X4),
+                    lhsT_scale=w2s[:, c0 : c0 + P],
+                    rhs=x_codes[a][:].bitcast(FP8X4),
+                    rhs_scale=x_sc[a][:],
+                    start=(a == 0),
+                    stop=(a == HP - 1),
+                )
+            if u in FUSED:
+                y_sb[u] = keep.tile([P, NP], F32, name=f"ysb{u}", tag=f"ysb{u}", align_bytes=64)
+                nc.scalar.copy(y_sb[u][:], ys[u][:])
         for gi, (u0, u1) in enumerate(GROUPS):
-            n = u1 - u0
-            logit = keep.tile([P, n, NP], F32, name=f"logit{gi}", tag=LOGIT_TAG[gi], align_bytes=64)
-            lik = keep.tile([P, n, NP], F32, name=f"lik{gi}", tag=f"big{gi}", align_bytes=64)
-            for b, t in (divmod(bt, PACK) for bt in range(u0, u1)):
-                y = psum.tile([P, BANK], F32, name=f"y{b}{t}", tag="acc")
-                for a in range(HP):
-                    c0 = a * H + b * PASS + t * P
-                    nc.tensor.matmul_mx(
-                        out=y[:],
-                        lhsT=w2w8[:, 2 * c0 : 2 * (c0 + P)].bitcast(FP4X4),
-                        lhsT_scale=w2s[:, c0 : c0 + P],
-                        rhs=x_codes[a][:].bitcast(FP8X4),
-                        rhs_scale=x_sc[a][:],
-                        start=(a == 0),
-                        stop=(a == HP - 1),
-                    )
-                u = PACK * b + t - u0
-                if (b, t) in FUSED:
-                    nc.scalar.copy(lik[:, u, :], y[:])
-                    nc.vector.tensor_tensor(logit[:, u, :], h[b, t][:].indirect(pos2_sb[:]), lik[:, u, :], ALU.mult)
+            for u in range(u0, u1):
+                b, t = divmod(u, PACK)
+                if u in FUSED:
+                    nc.vector.tensor_tensor(logit[:, u, :], h[b, t][:].indirect(pos2_sb[:]), y_sb[u][:], ALU.mult)
+                    last = y_sb[u][:]
                 else:
-                    nc.vector.tensor_copy(skip[t], h[b, t][:].indirect(pos2_sb[:]))
-                    nc.vector.tensor_tensor(logit[:, u, :], y[:], skip[t], ALU.mult)
+                    last = skip[u % len(skip)]
+                    nc.vector.tensor_copy(last, h[b, t][:].indirect(pos2_sb[:]))
+                    nc.vector.tensor_tensor(logit[:, u, :], ys[u][:], last, ALU.mult)
                 nc.scalar.activation(lik[:, u, :], logit[:, u, :], ACT.Sigmoid)
-            for c0, c1 in CUTS[gi]:
-                nc.scalar.activation(lik[:, :, c0:c1], lik[:, :, c0:c1], ACT.Ln, bias=floor[:])
-                nc.vector.tensor_tensor(lik[:, :, c0:c1], lik[:, :, c0:c1], logit[:, :, c0:c1], ALU.min)
-                for b in range(HP):
-                    lo, hi = max(u0, PACK * b), min(u1, PACK * (b + 1))
-                    if lo < hi:
-                        rows = out[b * PASS : (b + 1) * PASS, :].rearrange("(p t) m -> p t m", t=PACK)
-                        nc.sync.dma_start(rows[:, lo - PACK * b : hi - PACK * b, c0:c1], lik[:, lo - u0 : hi - u0, c0:c1])
+            if HOLD[gi] == "last":
+                bias = last[:, 0:1]
+                nc.gpsimd.memset(bias, FLOOR)
+            else:
+                bias = floor[:]
+            for v0, v1, c0, c1 in CUTS[gi]:
+                b = v0 // PACK
+                rows = out[b * PASS : (b + 1) * PASS, :].rearrange("(p t) m -> p t m", t=PACK)
+                nc.scalar.activation(lik[:, v0:v1, c0:c1], lik[:, v0:v1, c0:c1], ACT.Ln, bias=bias)
+                nc.vector.tensor_tensor(lik[:, v0:v1, c0:c1], lik[:, v0:v1, c0:c1], logit[:, v0:v1, c0:c1], ALU.min)
+                nc.sync.dma_start(rows[:, v0 - PACK * b : v1 - PACK * b, c0:c1], lik[:, v0:v1, c0:c1])

@@ -20,28 +20,18 @@ P = 128
 PACK = 4
 PASS = P * PACK
 BANK = 512
-KP = K // PASS
-HP = H // PASS
-FLOOR = 2.0**-60
-CASTS = {
-    (1, 0): (("v", 0, 128),),
-    (1, 1): (("s", 0, 32), ("s", 32, 64), ("s", 64, 96), ("s", 96, 128),),
-    (1, 2): (("v", 0, 64),("s", 64, 96), ("s", 96, 128),),
-    (0, 0): (("s", 0, 128),),
-    (0, 1): (("v", 0, 128),),
-    (0, 2): (("s", 0, 64), ("v", 64, 108), ("s", 108, 128)),
-}
-GORDER = ((0, 1, 2), (0, 1, 2))
-CUTS = (((0, 4, 0, 256), (0, 4, 256, 512)), ((4, 5, 0, 512), (5, 6, 0, 512), (6, 7, 0, 512), (7, 8, 0, 512),))
-LOGIT_TAG = ("big2", "raw10")
-FUSED = ()
-SILU_WEAVE = ()
-HOLD = ("none", "last")
-GAIN_S = ()
-WEAVE = (("s", 0, 32), ("s", 32, 64), ("s", 64, 96), ("s", 96, 128))
-SKIP_TAG = ("raw11", "raw12", (1, 2), "xb1")
-GAIN_G = ()
-GROUPS = ((0, 4), (4, 8))
+QUADRANTS = 4
+K_PASSES = K // PASS
+HALVES = H // PASS
+TILES = HALVES * PACK
+MX_ALIGN = 64
+
+CUTOFF = 42.0
+LATE_FLOOR = 2.0**-60
+
+VECTOR_ROUNDS = {(0, 1): (0, P), (0, 2): (64, 108), (1, 0): (0, P), (1, 2): (0, 64)}
+SCALAR_PIECE = 32
+VECTOR_GAINS = 320
 
 
 def tile_list_gazette_pair_loglik_kernel(
@@ -51,65 +41,68 @@ def tile_list_gazette_pair_loglik_kernel(
     with ExitStack() as ctx:
         lists = ctx.enter_context(tc.tile_pool(name="lists", bufs=1))
         keep = ctx.enter_context(tc.tile_pool(name="keep", bufs=1))
-        psum = ctx.enter_context(tc.psum_pool(name="psum", bufs=8))
+        psum = ctx.enter_context(tc.psum_pool(name="psum", bufs=TILES))
+
+        def room(shape, dtype, name, tag=None):
+            return keep.tile(shape, dtype, name=name, tag=tag or name, align_bytes=MX_ALIGN)
 
         offs_sb = lists.tile([P, S // 16], U16, name="offs_sb")
         pos1_sb = lists.tile([P, NP // 16], U16, name="pos1_sb")
         pos2_sb = lists.tile([P, NP // 16], U16, name="pos2_sb")
 
-        tab_sc = keep.tile([P, T], U8, name="tab_sc", align_bytes=64)
+        tab_sc = room([P, T], U8, "tab_sc")
         nc.vector.memset(tab_sc[:].bitcast(I32), 0)
-        w2s_raw = keep.tile([P, HP * H], U8, name="w2s_raw", align_bytes=64)
-        nc.vector.memset(w2s_raw[:].bitcast(I32), 0)
-        floor = keep.tile([P, 1], F32, name="floor")
-        nc.vector.memset(floor[:], FLOOR)
-        warm = keep.tile([P, 1], F32, name="warm")
-        nc.scalar.activation(warm[:], floor[:], ACT.Silu)
+        w2_sc_raw = room([P, HALVES * H], U8, "w2_sc_raw")
+        nc.vector.memset(w2_sc_raw[:].bitcast(I32), 0)
+        cutoff = keep.tile([P, 1], F32, name="cutoff")
+        nc.vector.memset(cutoff[:], CUTOFF)
+        nc.scalar.activation(cutoff[:], cutoff[:], ACT.Silu)
 
-        tab = [keep.tile([P, T], I32, name=f"tab{g}", tag=f"big{g}", align_bytes=64) for g in range(KP)]
+        tab = [room([P, T], I32, f"tab{g}") for g in range(K_PASSES)]
         w1_raw = {}
 
         def load_tab(g):
             nc.sync.dma_start(tab[g][:], tab_words[g].rearrange("p n i -> p (n i)").bitcast(I32))
 
         def load_w1(a, g, parts=1):
-            raw = keep.tile([P, PACK, PASS], F32, name=f"w1raw{a}{g}", tag=f"raw{a}{g}", align_bytes=64)
-            src = w1[g * PASS : (g + 1) * PASS, a * PASS : (a + 1) * PASS].rearrange("(p j) c -> p j c", j=PACK)
+            raw = room([P, PACK, PASS], F32, f"w1_raw{a}{g}")
+            block = w1[g * PASS : (g + 1) * PASS, a * PASS : (a + 1) * PASS].rearrange("(p j) c -> p j c", j=PACK)
             width = PASS // parts
             for c0 in range(0, PASS, width):
-                nc.sync.dma_start(raw[:, :, c0 : c0 + width], src[:, :, c0 : c0 + width])
+                nc.sync.dma_start(raw[:, :, c0 : c0 + width], block[:, :, c0 : c0 + width])
             w1_raw[a, g] = raw
 
         load_tab(0)
         nc.sync.dma_start(offs_sb[:], offs)
-        for q in range(4):
-            nc.gpsimd.dma_start(
-                tab_sc[32 * q : 32 * q + 4 * KP, :].bitcast(I32),
+        for q in range(QUADRANTS):
+            queue = nc.gpsimd if q < QUADRANTS - 1 else nc.scalar
+            queue.dma_start(
+                tab_sc[32 * q : 32 * q + 4 * K_PASSES, :].bitcast(I32),
                 tab_scales[:, 4 * q : 4 * q + 4, :].bitcast(I32),
             )
-        w2w_raw = keep.tile([P, HP, H // 2], I32, name="w2w_raw", align_bytes=64)
-        nc.sync.dma_start(w2w_raw[:], w2_words.bitcast(I32).rearrange("a p w -> p a w"))
+        w2_raw = room([P, HALVES, H // 2], I32, "w2_raw")
+        nc.sync.dma_start(w2_raw[:], w2_words.bitcast(I32).rearrange("a p w -> p a w"))
         nc.sync.dma_start(pos1_sb[:], pos1)
         nc.sync.dma_start(pos2_sb[:], pos2)
-        b1_sb = keep.tile([P, HP, PACK], F32, name="b1_sb")
-        nc.scalar.dma_start(b1_sb[:], b1.rearrange("(a p t) -> p a t", a=HP, t=PACK))
-        gain_sb = keep.tile([P, HP, PACK], F32, name="gain_sb")
-        nc.scalar.dma_start(gain_sb[:], gain.rearrange("(a p t) -> p a t", a=HP, t=PACK))
+        b1_sb = keep.tile([P, HALVES, PACK], F32, name="b1_sb")
+        nc.scalar.dma_start(b1_sb[:], b1.rearrange("(a p t) -> p a t", a=HALVES, t=PACK))
+        gain_sb = keep.tile([P, HALVES, PACK], F32, name="gain_sb")
+        nc.scalar.dma_start(gain_sb[:], gain.rearrange("(a p t) -> p a t", a=HALVES, t=PACK))
         load_tab(1)
-        for q in range(4):
+        for q in range(QUADRANTS):
             nc.sync.dma_start(
-                w2s_raw[32 * q : 32 * q + 4, :].bitcast(I32).rearrange("r (a w) -> r a w", a=HP),
+                w2_sc_raw[32 * q : 32 * q + 4, :].bitcast(I32).rearrange("r (a w) -> r a w", a=HALVES),
                 w2_scales[:, 4 * q : 4 * q + 4, :].bitcast(I32).rearrange("a r w -> r a w"),
             )
         load_w1(0, 0)
         load_tab(2)
         load_w1(0, 1)
         load_w1(0, 2, parts=2)
-        for g in range(KP):
+        for g in range(K_PASSES):
             load_w1(1, g)
 
-        v_words = [keep.tile([P, S], U32, name=f"vw{g}", align_bytes=64) for g in range(KP)]
-        v_sc = keep.tile([P, S], U8, name="v_sc", align_bytes=64)
+        v_words = [room([P, S], U32, f"v_words{g}") for g in range(K_PASSES)]
+        v_sc = room([P, S], U8, "v_sc")
 
         def gather_words(g):
             nc.vector.tensor_copy(v_words[g][:], tab[g][:].bitcast(U32).indirect(offs_sb[:]))
@@ -117,111 +110,80 @@ def tile_list_gazette_pair_loglik_kernel(
         w1_codes, w1_sc = {}, {}
 
         def quantise_w1(a, g, parts=1):
-            grouped = keep.tile([P, PASS * PACK], BF16, name=f"grp{a}{g}", tag=f"grp{g}", align_bytes=64)
-            dst = grouped[:].rearrange("p (t m j) -> p m j t", t=PACK, j=PACK)
+            rounded = room([P, PASS * PACK], BF16, f"w1_rounded{a}{g}", tag=f"rounded{g}")
+            dst = rounded[:].rearrange("p (t m j) -> p m j t", t=PACK, j=PACK)
             src = w1_raw[a, g][:].rearrange("p j (m t) -> p m j t", t=PACK)
-            for eng, m0, m1 in CASTS[a, g]:
-                if eng == "v":
-                    nc.vector.tensor_copy(dst[:, m0:m1], src[:, m0:m1])
-                elif eng == "s":
-                    nc.scalar.copy(dst[:, m0:m1], src[:, m0:m1])
-                else:
-                    nc.gpsimd.tensor_scalar(dst[:, m0:m1], src[:, m0:m1], 1.0, 0.0, ALU.mult, ALU.add)
-            codes = keep.tile([P, PASS], U32, name=f"w1c{a}{g}", align_bytes=64)
-            scales = keep.tile([P, PASS], U8, name=f"w1s{a}{g}", align_bytes=64)
+            v0, v1 = VECTOR_ROUNDS.get((a, g), (P, P))
+            piece = P if a == 0 else SCALAR_PIECE
+            for m0 in range(0, v0, piece):
+                nc.scalar.copy(dst[:, m0 : min(m0 + piece, v0)], src[:, m0 : min(m0 + piece, v0)])
+            if v0 < v1:
+                nc.vector.tensor_copy(dst[:, v0:v1], src[:, v0:v1])
+            for m0 in range(v1, P, piece):
+                nc.scalar.copy(dst[:, m0 : min(m0 + piece, P)], src[:, m0 : min(m0 + piece, P)])
+            codes = room([P, PASS], U32, f"w1_codes{a}{g}")
+            scales = room([P, PASS], U8, f"w1_sc{a}{g}")
             width = PASS // parts
             for c0 in range(0, PASS, width):
                 nc.vector.quantize_mx(
                     out=codes[:, c0 : c0 + width].bitcast(FP8X4),
                     scales=scales[:, c0 : c0 + width],
-                    in_=grouped[:, PACK * c0 : PACK * (c0 + width)],
+                    in_=rounded[:, PACK * c0 : PACK * (c0 + width)],
                 )
             w1_codes[a, g], w1_sc[a, g] = codes, scales
 
-        h_acc = {}
+        h_sums = {}
 
-        def first_product(a, i, t):
-            g = GORDER[a][i]
-            for nh in range(S // BANK):
-                if i == 0:
-                    h_acc[a, t, nh] = psum.tile([P, BANK], F32, name=f"hacc{a}{t}{nh}", tag="acc")
+        def first_product(a, g, t):
+            for c0 in range(0, S, BANK):
+                if g == 0:
+                    h_sums[a, t, c0] = psum.tile([P, BANK], F32, name=f"h_sums{a}{t}_{c0}", tag="bank")
                 nc.tensor.matmul_mx(
-                    out=h_acc[a, t, nh][:],
+                    out=h_sums[a, t, c0][:],
                     lhsT=w1_codes[a, g][:, t * P : (t + 1) * P].bitcast(FP8X4),
                     lhsT_scale=w1_sc[a, g][:, t * P : (t + 1) * P],
-                    rhs=v_words[g][:, nh * BANK : (nh + 1) * BANK].bitcast(FP8X4),
-                    rhs_scale=v_sc[4 * g :, nh * BANK : (nh + 1) * BANK],
-                    start=(i == 0),
-                    stop=(i == KP - 1),
+                    rhs=v_words[g][:, c0 : c0 + BANK].bitcast(FP8X4),
+                    rhs_scale=v_sc[4 * g :, c0 : c0 + BANK],
+                    start=(g == 0),
+                    stop=(g == K_PASSES - 1),
                 )
 
         h = {}
 
-        def leave_psum(a, t):
+        def add_bias(a, t):
             h[a, t] = keep.tile([P, S], F32, name=f"h{a}{t}")
-            for nh in range(S // BANK):
-                dst = h[a, t][:, nh * BANK : (nh + 1) * BANK]
-                if (a, t, nh) == (0, 0, 1):
-                    nc.vector.tensor_scalar(dst, h_acc[a, t, nh][:], b1_sb[:, a, t : t + 1], None, ALU.add)
-                else:
-                    nc.scalar.activation(dst, h_acc[a, t, nh][:], ACT.Identity, bias=b1_sb[:, a, t : t + 1])
+            for c0 in range(0, S, BANK):
+                nc.scalar.activation(
+                    h[a, t][:, c0 : c0 + BANK], h_sums[a, t, c0][:], ACT.Identity, bias=b1_sb[:, a, t : t + 1]
+                )
 
-        old = {}
+        old, silu = {}, {}
 
-        def pick_old(a, t):
+        def gather_old(a, t):
             if t == 0:
-                old[a] = keep.tile([P, PACK, NP], F32, name=f"old{a}", tag=f"pick{a}", align_bytes=64)
+                old[a] = room([P, PACK, NP], F32, f"old{a}")
             nc.vector.tensor_copy(old[a][:, t, :], h[a, t][:].indirect(pos1_sb[:]))
-
-        act = {}
 
         def silu_old(a, t):
             if t == 0:
-                act[a] = keep.tile([P, PACK, NP], F32, name=f"act{a}", tag=f"raw0{a}", align_bytes=64)
-            if not SILU_WEAVE:
-                nc.scalar.activation(act[a][:, t, :], old[a][:, t, :], ACT.Silu)
-            elif t == PACK - 1:
-                dst = act[a][:].rearrange("p t m -> p (t m)").rearrange("p (c i t) -> p c t i", i=4, t=PACK)
-                src = old[a][:].rearrange("p t (c i) -> p c t i", i=4)
-                for c0, c1 in SILU_WEAVE:
-                    nc.scalar.activation(dst[:, c0:c1], src[:, c0:c1], ACT.Silu)
+                silu[a] = room([P, PACK, NP], F32, f"silu{a}", tag=f"w1_raw0{a}")
+            nc.scalar.activation(silu[a][:, t, :], old[a][:, t, :], ACT.Silu)
 
-        x_codes, x_sc = {}, {}
+        x_rounded, x_codes, x_sc = {}, {}, {}
 
-        def make_x(a):
-            xb = keep.tile([P, NP * PACK], BF16, name=f"xb{a}", tag=f"xb{a}", align_bytes=64)
-            if a in GAIN_S:
-                xp = keep.tile([P, PACK, NP], BF16, name=f"xp{a}", tag="grp0", align_bytes=64)
-                for t in range(PACK):
-                    nc.scalar.activation(xp[:, t, :], act[a][:, t, :], ACT.Copy, scale=gain_sb[:, a, t : t + 1])
-                for eng, c0, c1 in WEAVE:
-                    dst = xb[:].rearrange("p (c i t) -> p c t i", i=4, t=PACK)[:, c0:c1]
-                    src = xp[:].rearrange("p t (c i) -> p c t i", i=4)[:, c0:c1]
-                    if eng == "s":
-                        nc.scalar.copy(dst, src)
-                    else:
-                        nc.vector.tensor_copy(dst, src)
-            elif SILU_WEAVE:
-                dst = xb[:].rearrange("p (m t) -> p m t", t=PACK)
-                src = act[a][:].rearrange("p t m -> p (t m)").rearrange("p (m t) -> p m t", t=PACK)
-                for c0, c1 in SILU_WEAVE:
-                    nc.vector.tensor_tensor(
-                        dst[:, 4 * c0 : 4 * c1],
-                        src[:, 4 * c0 : 4 * c1],
-                        gain_sb[:, a, :].unsqueeze(1).to_broadcast([P, 4 * (c1 - c0), PACK]),
-                        ALU.mult,
-                    )
-            else:
-                eng = nc.gpsimd if a in GAIN_G else nc.vector
-                eng.tensor_tensor(
-                    xb[:].rearrange("p (c i t) -> p c t i", i=2, t=PACK),
-                    act[a][:].rearrange("p t (c i) -> p c t i", i=2),
-                    gain_sb[:, a, :].unsqueeze(1).unsqueeze(3).to_broadcast([P, NP // 2, PACK, 2]),
-                    ALU.mult,
-                )
-            x_codes[a] = keep.tile([P, NP], U32, name=f"xc{a}", align_bytes=64)
-            x_sc[a] = keep.tile([P, NP], U8, name=f"xs{a}", align_bytes=64)
-            nc.vector.quantize_mx(out=x_codes[a][:].bitcast(FP8X4), scales=x_sc[a][:], in_=xb[:])
+        def gain_on_vector(a, columns):
+            x_rounded[a] = room([P, NP * PACK], BF16, f"x_rounded{a}")
+            nc.vector.tensor_tensor(
+                x_rounded[a][:].rearrange("p (c i t) -> p c t i", i=2, t=PACK)[:, : columns // 2],
+                silu[a][:].rearrange("p t (c i) -> p c t i", i=2)[:, : columns // 2],
+                gain_sb[:, a, :].unsqueeze(1).unsqueeze(3).to_broadcast([P, columns // 2, PACK, 2]),
+                ALU.mult,
+            )
+
+        def quantise_x(a):
+            x_codes[a] = room([P, NP], U32, f"x_codes{a}")
+            x_sc[a] = room([P, NP], U8, f"x_sc{a}")
+            nc.vector.quantize_mx(out=x_codes[a][:].bitcast(FP8X4), scales=x_sc[a][:], in_=x_rounded[a][:])
 
         gather_words(0)
         nc.vector.tensor_copy(v_sc[:], tab_sc[:].indirect(offs_sb[:]))
@@ -235,86 +197,102 @@ def tile_list_gazette_pair_loglik_kernel(
         for t in range(PACK):
             first_product(0, 1, t)
             first_product(0, 2, t)
-            leave_psum(0, t)
+            add_bias(0, t)
 
-        w2w = keep.tile([P, HP * H], U16, name="w2w", align_bytes=64)
+        w2_codes = room([P, HALVES * H], U16, "w2_codes")
         nc.vector.tensor_copy(
-            w2w[:].rearrange("p (ab t m) -> p ab t m", t=PACK, m=P),
-            w2w_raw[:].rearrange("p a w -> p (a w)").bitcast(U16).rearrange("p (ab m t) -> p ab t m", t=PACK, m=P),
+            w2_codes[:].rearrange("p (ab t m) -> p ab t m", t=PACK, m=P),
+            w2_raw[:].rearrange("p a w -> p (a w)").bitcast(U16).rearrange("p (ab m t) -> p ab t m", t=PACK, m=P),
         )
-        w2s = keep.tile([P, HP * H], U8, name="w2s", align_bytes=64)
+        w2_sc = room([P, HALVES * H], U8, "w2_sc")
         nc.vector.tensor_copy(
-            w2s[:].rearrange("p (ab t m) -> p ab t m", t=PACK, m=P),
-            w2s_raw[:].rearrange("p (ab m t) -> p ab t m", t=PACK, m=P),
+            w2_sc[:].rearrange("p (ab t m) -> p ab t m", t=PACK, m=P),
+            w2_sc_raw[:].rearrange("p (ab m t) -> p ab t m", t=PACK, m=P),
         )
 
         for t in range(PACK):
-            pick_old(0, t)
-        for g in range(KP):
+            gather_old(0, t)
+        for g in range(K_PASSES):
             quantise_w1(1, g)
-        for i in range(KP - 1):
+        for g in range(K_PASSES - 1):
             for t in range(PACK):
-                first_product(1, i, t)
+                first_product(1, g, t)
         for t in range(PACK):
-            first_product(1, KP - 1, t)
-            leave_psum(1, t)
+            first_product(1, K_PASSES - 1, t)
+            add_bias(1, t)
         for t in range(PACK):
             silu_old(0, t)
+        x_rows = room([P, PACK, NP - VECTOR_GAINS], BF16, "x_rows", tag="rounded0")
         for t in range(PACK):
-            pick_old(1, t)
+            gather_old(1, t)
             silu_old(1, t)
-        make_x(0)
-        make_x(1)
-        warm2 = keep.tile([P, 1], F32, name="warm2")
-        nc.scalar.activation(warm2[:], act[1][:, PACK - 1, NP - 1 : NP], ACT.Sigmoid)
+            nc.scalar.activation(
+                x_rows[:, t, :], silu[1][:, t, VECTOR_GAINS:], ACT.Copy, scale=gain_sb[:, 1, t : t + 1]
+            )
+        gain_on_vector(0, NP)
+        quantise_x(0)
+        gain_on_vector(1, VECTOR_GAINS)
+        nc.scalar.copy(
+            x_rounded[1][:].rearrange("p (c i t) -> p c t i", i=4, t=PACK)[:, VECTOR_GAINS // 4 :],
+            x_rows[:].rearrange("p t (c i) -> p c t i", i=4),
+        )
+        quantise_x(1)
+        floor = room([P, 1], F32, "floor", tag="rounded0")
+        nc.scalar.activation(floor[:], cutoff[:], ACT.Sigmoid, scale=-1.0)
 
-        w2w8 = w2w[:].bitcast(U8)
-        skip = []
-        for t, tag in enumerate(SKIP_TAG):
-            if isinstance(tag, str):
-                room = keep.tile([P, NP], F32, name=f"skip{t}", tag=tag, align_bytes=64)
-                skip.append(room[:])
-            else:
-                skip.append(old[tag[0]][:, tag[1], :])
-        logit = keep.tile([P, HP * PACK, NP], F32, name="logit", tag="big0", align_bytes=64)
-        lik = keep.tile([P, HP * PACK, NP], F32, name="lik", tag="big1", align_bytes=64)
-        ys, y_sb = {}, {}
-        for u in range(HP * PACK):
-            b, t = divmod(u, PACK)
-            ys[u] = psum.tile([P, BANK], F32, name=f"y{u}", tag="acc")
-            for a in range(HP):
-                c0 = a * H + b * PASS + t * P
+        w2_bytes = w2_codes[:].bitcast(U8)
+        skip_0 = room([P, NP], F32, "skip_0", tag="w1_raw11")
+        skip_1 = room([P, NP], F32, "skip_1", tag="w1_raw12")
+        skip_3 = room([P, NP], F32, "skip_3", tag="x_rounded1")
+        skip = [skip_0[:], skip_1[:], old[1][:, 2, :], skip_3[:]]
+        logit = room([P, TILES, NP], F32, "logit", tag="tab0")
+        result = room([P, TILES, NP], F32, "result", tag="tab1")
+        y = []
+        for u in range(TILES):
+            y.append(psum.tile([P, BANK], F32, name=f"y{u}", tag="bank"))
+            for a in range(HALVES):
+                c0 = a * H + u * P
                 nc.tensor.matmul_mx(
-                    out=ys[u][:],
-                    lhsT=w2w8[:, 2 * c0 : 2 * (c0 + P)].bitcast(FP4X4),
-                    lhsT_scale=w2s[:, c0 : c0 + P],
+                    out=y[u][:],
+                    lhsT=w2_bytes[:, 2 * c0 : 2 * (c0 + P)].bitcast(FP4X4),
+                    lhsT_scale=w2_sc[:, c0 : c0 + P],
                     rhs=x_codes[a][:].bitcast(FP8X4),
                     rhs_scale=x_sc[a][:],
                     start=(a == 0),
-                    stop=(a == HP - 1),
+                    stop=(a == HALVES - 1),
                 )
-            if u in FUSED:
-                y_sb[u] = keep.tile([P, NP], F32, name=f"ysb{u}", tag=f"ysb{u}", align_bytes=64)
-                nc.scalar.copy(y_sb[u][:], ys[u][:])
-        for gi, (u0, u1) in enumerate(GROUPS):
-            for u in range(u0, u1):
-                b, t = divmod(u, PACK)
-                if u in FUSED:
-                    nc.vector.tensor_tensor(logit[:, u, :], h[b, t][:].indirect(pos2_sb[:]), y_sb[u][:], ALU.mult)
-                    last = y_sb[u][:]
-                else:
-                    last = skip[u % len(skip)]
-                    nc.vector.tensor_copy(last, h[b, t][:].indirect(pos2_sb[:]))
-                    nc.vector.tensor_tensor(logit[:, u, :], ys[u][:], last, ALU.mult)
-                nc.scalar.activation(lik[:, u, :], logit[:, u, :], ACT.Sigmoid)
-            if HOLD[gi] == "last":
-                bias = last[:, 0:1]
-                nc.gpsimd.memset(bias, FLOOR)
-            else:
-                bias = floor[:]
-            for v0, v1, c0, c1 in CUTS[gi]:
-                b = v0 // PACK
-                rows = out[b * PASS : (b + 1) * PASS, :].rearrange("(p t) m -> p t m", t=PACK)
-                nc.scalar.activation(lik[:, v0:v1, c0:c1], lik[:, v0:v1, c0:c1], ACT.Ln, bias=bias)
-                nc.vector.tensor_tensor(lik[:, v0:v1, c0:c1], lik[:, v0:v1, c0:c1], logit[:, v0:v1, c0:c1], ALU.min)
-                nc.sync.dma_start(rows[:, v0 - PACK * b : v1 - PACK * b, c0:c1], lik[:, v0:v1, c0:c1])
+
+        def logits(u):
+            nc.vector.tensor_copy(skip[u % PACK], h[divmod(u, PACK)][:].indirect(pos2_sb[:]))
+            nc.vector.tensor_tensor(logit[:, u, :], y[u][:], skip[u % PACK], ALU.mult)
+
+        def sigmoid(u):
+            nc.scalar.activation(result[:, u, :], logit[:, u, :], ACT.Sigmoid)
+
+        def log_of(tiles, cols, bias):
+            nc.scalar.activation(result[:, tiles, cols], result[:, tiles, cols], ACT.Ln, bias=bias)
+
+        def finish(tiles, cols):
+            b = tiles.start // PACK
+            rows = out[b * PASS : (b + 1) * PASS, :].rearrange("(p t) m -> p t m", t=PACK)
+            nc.vector.tensor_tensor(result[:, tiles, cols], result[:, tiles, cols], logit[:, tiles, cols], ALU.min)
+            nc.sync.dma_start(rows[:, tiles.start - PACK * b : tiles.stop - PACK * b, cols], result[:, tiles, cols])
+
+        first_tiles = slice(0, PACK)
+        column_halves = (slice(0, NP // 2), slice(NP // 2, NP))
+        for u in range(PACK):
+            logits(u)
+            sigmoid(u)
+        for cols in column_halves:
+            log_of(first_tiles, cols, floor[:])
+        for u in range(PACK, TILES):
+            logits(u)
+        for cols in column_halves:
+            finish(first_tiles, cols)
+        for u in range(PACK, TILES):
+            sigmoid(u)
+        late_floor = skip[PACK - 1][:, 0:1]
+        nc.gpsimd.memset(late_floor, LATE_FLOOR)
+        for u in range(PACK, TILES):
+            log_of(slice(u, u + 1), slice(0, NP), late_floor)
+            finish(slice(u, u + 1), slice(0, NP))

@@ -29,7 +29,7 @@ MX_ALIGN = 64
 CUTOFF = 42.0
 LATE_FLOOR = 2.0**-60
 
-VECTOR_ROUNDS = {(0, 1): (0, P), (0, 2): (64, 108), (1, 0): (0, P), (1, 2): (0, 64)}
+VECTOR_QUARTERS = ((0, 3, 3), (4, 1, 2))
 SCALAR_PIECE = 32
 VECTOR_GAINS = 320
 
@@ -113,14 +113,15 @@ def tile_list_gazette_pair_loglik_kernel(
             rounded = room([P, PASS * PACK], BF16, f"w1_rounded{a}{g}", tag=f"rounded{g}")
             dst = rounded[:].rearrange("p (t m j) -> p m j t", t=PACK, j=PACK)
             src = w1_raw[a, g][:].rearrange("p j (m t) -> p m j t", t=PACK)
-            v0, v1 = VECTOR_ROUNDS.get((a, g), (P, P))
-            piece = P if a == 0 else SCALAR_PIECE
-            for m0 in range(0, v0, piece):
-                nc.scalar.copy(dst[:, m0 : min(m0 + piece, v0)], src[:, m0 : min(m0 + piece, v0)])
-            if v0 < v1:
-                nc.vector.tensor_copy(dst[:, v0:v1], src[:, v0:v1])
-            for m0 in range(v1, P, piece):
-                nc.scalar.copy(dst[:, m0 : min(m0 + piece, P)], src[:, m0 : min(m0 + piece, P)])
+            part = P // parts
+            for m0 in range(0, P, part):
+                split = m0 + part * VECTOR_QUARTERS[a][g] // 4
+                if split > m0:
+                    nc.vector.tensor_copy(dst[:, m0:split], src[:, m0:split])
+                piece = SCALAR_PIECE if a == 1 else part
+                for s0 in range(split, m0 + part, piece):
+                    s1 = min(s0 + piece, m0 + part)
+                    nc.scalar.copy(dst[:, s0:s1], src[:, s0:s1])
             codes = room([P, PASS], U32, f"w1_codes{a}{g}")
             scales = room([P, PASS], U8, f"w1_sc{a}{g}")
             width = PASS // parts

from contextlib import ExitStack

import concourse.mybir as mybir

K, H, T, S, NP = 1536, 1024, 4096, 1024, 512
FLOPS = 2 * K * H * S + 2 * H * H * NP

F32 = mybir.dt.float32
BF16 = mybir.dt.bfloat16
I32 = mybir.dt.int32
U32 = mybir.dt.uint32
U16 = mybir.dt.uint16
U8 = mybir.dt.uint8
FP8X4 = mybir.dt.float8_e4m3fn_x4
FP4X4 = mybir.dt.float4_e2m1fn_x4
ACT = mybir.ActivationFunctionType
ALU = mybir.AluOpType

P = 128
PACK = 4
PASS = P * PACK
BANK = 512
QUADRANTS = 4
K_PASSES = K // PASS
HALVES = H // PASS
TILES = HALVES * PACK
MX_ALIGN = 64

CUTOFF = 42.0
LATE_FLOOR = 2.0**-60

VECTOR_QUARTERS = ((0, 3, 3), (4, 1, 2))
SCALAR_PIECE = 32
VECTOR_GAINS = 320


def tile_list_gazette_pair_loglik_kernel(
    tc, tab_words, tab_scales, offs, pos1, pos2, w1, b1, gain, w2_words, w2_scales, out
):
    nc = tc.nc
    with ExitStack() as ctx:
        lists = ctx.enter_context(tc.tile_pool(name="lists", bufs=1))
        keep = ctx.enter_context(tc.tile_pool(name="keep", bufs=1))
        psum = ctx.enter_context(tc.psum_pool(name="psum", bufs=TILES))

        def room(shape, dtype, name, tag=None):
            return keep.tile(shape, dtype, name=name, tag=tag or name, align_bytes=MX_ALIGN)

        offs_sb = lists.tile([P, S // 16], U16, name="offs_sb")
        pos1_sb = lists.tile([P, NP // 16], U16, name="pos1_sb")
        pos2_sb = lists.tile([P, NP // 16], U16, name="pos2_sb")

        tab_sc = room([P, T], U8, "tab_sc")
        nc.vector.memset(tab_sc[:].bitcast(I32), 0)
        w2_sc_raw = room([P, HALVES * H], U8, "w2_sc_raw")
        nc.vector.memset(w2_sc_raw[:].bitcast(I32), 0)
        cutoff = keep.tile([P, 1], F32, name="cutoff")
        nc.vector.memset(cutoff[:], CUTOFF)
        nc.scalar.activation(cutoff[:], cutoff[:], ACT.Silu)

        tab = [room([P, T], I32, f"tab{g}") for g in range(K_PASSES)]
        w1_raw = {}

        def load_tab(g):
            nc.sync.dma_start(tab[g][:], tab_words[g].rearrange("p n i -> p (n i)").bitcast(I32))

        def load_w1(a, g, parts=1):
            raw = room([P, PACK, PASS], F32, f"w1_raw{a}{g}")
            block = w1[g * PASS : (g + 1) * PASS, a * PASS : (a + 1) * PASS].rearrange("(p j) c -> p j c", j=PACK)
            width = PASS // parts
            for c0 in range(0, PASS, width):
                nc.sync.dma_start(raw[:, :, c0 : c0 + width], block[:, :, c0 : c0 + width])
            w1_raw[a, g] = raw

        load_tab(0)
        nc.sync.dma_start(offs_sb[:], offs)
        for q in range(QUADRANTS):
            queue = nc.gpsimd if q < QUADRANTS - 1 else nc.scalar
            queue.dma_start(
                tab_sc[32 * q : 32 * q + 4 * K_PASSES, :].bitcast(I32),
                tab_scales[:, 4 * q : 4 * q + 4, :].bitcast(I32),
            )
        w2_raw = room([P, HALVES, H // 2], I32, "w2_raw")
        nc.sync.dma_start(w2_raw[:], w2_words.bitcast(I32).rearrange("a p w -> p a w"))
        nc.sync.dma_start(pos1_sb[:], pos1)
        nc.sync.dma_start(pos2_sb[:], pos2)
        b1_sb = keep.tile([P, HALVES, PACK], F32, name="b1_sb")
        nc.scalar.dma_start(b1_sb[:], b1.rearrange("(a p t) -> p a t", a=HALVES, t=PACK))
        gain_sb = keep.tile([P, HALVES, PACK], F32, name="gain_sb")
        nc.scalar.dma_start(gain_sb[:], gain.rearrange("(a p t) -> p a t", a=HALVES, t=PACK))
        load_tab(1)
        for q in range(QUADRANTS):
            nc.sync.dma_start(
                w2_sc_raw[32 * q : 32 * q + 4, :].bitcast(I32).rearrange("r (a w) -> r a w", a=HALVES),
                w2_scales[:, 4 * q : 4 * q + 4, :].bitcast(I32).rearrange("a r w -> r a w"),
            )
        load_w1(0, 0)
        load_tab(2)
        load_w1(0, 1)
        load_w1(0, 2, parts=2)
        for g in range(K_PASSES):
            load_w1(1, g)

        v_words = [room([P, S], U32, f"v_words{g}") for g in range(K_PASSES)]
        v_sc = room([P, S], U8, "v_sc")

        def gather_words(g):
            nc.vector.tensor_copy(v_words[g][:], tab[g][:].bitcast(U32).indirect(offs_sb[:]))

        w1_codes, w1_sc = {}, {}

        def quantise_w1(a, g, parts=1):
            rounded = room([P, PASS * PACK], BF16, f"w1_rounded{a}{g}", tag=f"rounded{g}")
            dst = rounded[:].rearrange("p (t m j) -> p m j t", t=PACK, j=PACK)
            src = w1_raw[a, g][:].rearrange("p j (m t) -> p m j t", t=PACK)
            part = P // parts
            for m0 in range(0, P, part):
                split = m0 + part * VECTOR_QUARTERS[a][g] // 4
                if split > m0:
                    nc.vector.tensor_copy(dst[:, m0:split], src[:, m0:split])
                piece = SCALAR_PIECE if a == 1 else part
                for s0 in range(split, m0 + part, piece):
                    s1 = min(s0 + piece, m0 + part)
                    nc.scalar.copy(dst[:, s0:s1], src[:, s0:s1])
            codes = room([P, PASS], U32, f"w1_codes{a}{g}")
            scales = room([P, PASS], U8, f"w1_sc{a}{g}")
            width = PASS // parts
            for c0 in range(0, PASS, width):
                nc.vector.quantize_mx(
                    out=codes[:, c0 : c0 + width].bitcast(FP8X4),
                    scales=scales[:, c0 : c0 + width],
                    in_=rounded[:, PACK * c0 : PACK * (c0 + width)],
                )
            w1_codes[a, g], w1_sc[a, g] = codes, scales

        h_sums = {}

        def first_product(a, g, t):
            for c0 in range(0, S, BANK):
                if g == 0:
                    h_sums[a, t, c0] = psum.tile([P, BANK], F32, name=f"h_sums{a}{t}_{c0}", tag="bank")
                nc.tensor.matmul_mx(
                    out=h_sums[a, t, c0][:],
                    lhsT=w1_codes[a, g][:, t * P : (t + 1) * P].bitcast(FP8X4),
                    lhsT_scale=w1_sc[a, g][:, t * P : (t + 1) * P],
                    rhs=v_words[g][:, c0 : c0 + BANK].bitcast(FP8X4),
                    rhs_scale=v_sc[4 * g :, c0 : c0 + BANK],
                    start=(g == 0),
                    stop=(g == K_PASSES - 1),
                )

        h = {}

        def add_bias(a, t):
            h[a, t] = keep.tile([P, S], F32, name=f"h{a}{t}")
            for c0 in range(0, S, BANK):
                nc.scalar.activation(
                    h[a, t][:, c0 : c0 + BANK], h_sums[a, t, c0][:], ACT.Identity, bias=b1_sb[:, a, t : t + 1]
                )

        old, silu = {}, {}

        def gather_old(a, t):
            if t == 0:
                old[a] = room([P, PACK, NP], F32, f"old{a}")
            nc.vector.tensor_copy(old[a][:, t, :], h[a, t][:].indirect(pos1_sb[:]))

        def silu_old(a, t):
            if t == 0:
                silu[a] = room([P, PACK, NP], F32, f"silu{a}", tag=f"w1_raw0{a}")
            nc.scalar.activation(silu[a][:, t, :], old[a][:, t, :], ACT.Silu)

        x_rounded, x_codes, x_sc = {}, {}, {}

        def gain_on_vector(a, columns):
            x_rounded[a] = room([P, NP * PACK], BF16, f"x_rounded{a}")
            nc.vector.tensor_tensor(
                x_rounded[a][:].rearrange("p (c i t) -> p c t i", i=2, t=PACK)[:, : columns // 2],
                silu[a][:].rearrange("p t (c i) -> p c t i", i=2)[:, : columns // 2],
                gain_sb[:, a, :].unsqueeze(1).unsqueeze(3).to_broadcast([P, columns // 2, PACK, 2]),
                ALU.mult,
            )

        def quantise_x(a):
            x_codes[a] = room([P, NP], U32, f"x_codes{a}")
            x_sc[a] = room([P, NP], U8, f"x_sc{a}")
            nc.vector.quantize_mx(out=x_codes[a][:].bitcast(FP8X4), scales=x_sc[a][:], in_=x_rounded[a][:])

        gather_words(0)
        nc.vector.tensor_copy(v_sc[:], tab_sc[:].indirect(offs_sb[:]))
        gather_words(1)
        gather_words(2)
        quantise_w1(0, 0)
        for t in range(PACK):
            first_product(0, 0, t)
        quantise_w1(0, 1)
        quantise_w1(0, 2, parts=2)
        for t in range(PACK):
            first_product(0, 1, t)
            first_product(0, 2, t)
            add_bias(0, t)

        w2_codes = room([P, HALVES * H], U16, "w2_codes")
        nc.vector.tensor_copy(
            w2_codes[:].rearrange("p (ab t m) -> p ab t m", t=PACK, m=P),
            w2_raw[:].rearrange("p a w -> p (a w)").bitcast(U16).rearrange("p (ab m t) -> p ab t m", t=PACK, m=P),
        )
        w2_sc = room([P, HALVES * H], U8, "w2_sc")
        nc.vector.tensor_copy(
            w2_sc[:].rearrange("p (ab t m) -> p ab t m", t=PACK, m=P),
            w2_sc_raw[:].rearrange("p (ab m t) -> p ab t m", t=PACK, m=P),
        )

        for t in range(PACK):
            gather_old(0, t)
        for g in range(K_PASSES):
            quantise_w1(1, g)
        for g in range(K_PASSES - 1):
            for t in range(PACK):
                first_product(1, g, t)
        for t in range(PACK):
            first_product(1, K_PASSES - 1, t)
            add_bias(1, t)
        for t in range(PACK):
            silu_old(0, t)
        x_rows = room([P, PACK, NP - VECTOR_GAINS], BF16, "x_rows", tag="rounded0")
        for t in range(PACK):
            gather_old(1, t)
            silu_old(1, t)
            nc.scalar.activation(
                x_rows[:, t, :], silu[1][:, t, VECTOR_GAINS:], ACT.Copy, scale=gain_sb[:, 1, t : t + 1]
            )
        gain_on_vector(0, NP)
        quantise_x(0)
        gain_on_vector(1, VECTOR_GAINS)
        nc.scalar.copy(
            x_rounded[1][:].rearrange("p (c i t) -> p c t i", i=4, t=PACK)[:, VECTOR_GAINS // 4 :],
            x_rows[:].rearrange("p t (c i) -> p c t i", i=4),
        )
        quantise_x(1)
        floor = room([P, 1], F32, "floor", tag="rounded0")
        nc.scalar.activation(floor[:], cutoff[:], ACT.Sigmoid, scale=-1.0)

        w2_bytes = w2_codes[:].bitcast(U8)
        skip_0 = room([P, NP], F32, "skip_0", tag="w1_raw11")
        skip_1 = room([P, NP], F32, "skip_1", tag="w1_raw12")
        skip_3 = room([P, NP], F32, "skip_3", tag="x_rounded1")
        skip = [skip_0[:], skip_1[:], old[1][:, 2, :], skip_3[:]]
        logit = room([P, TILES, NP], F32, "logit", tag="tab0")
        result = room([P, TILES, NP], F32, "result", tag="tab1")
        y = []
        for u in range(TILES):
            y.append(psum.tile([P, BANK], F32, name=f"y{u}", tag="bank"))
            for a in range(HALVES):
                c0 = a * H + u * P
                nc.tensor.matmul_mx(
                    out=y[u][:],
                    lhsT=w2_bytes[:, 2 * c0 : 2 * (c0 + P)].bitcast(FP4X4),
                    lhsT_scale=w2_sc[:, c0 : c0 + P],
                    rhs=x_codes[a][:].bitcast(FP8X4),
                    rhs_scale=x_sc[a][:],
                    start=(a == 0),
                    stop=(a == HALVES - 1),
                )

        def logits(u):
            nc.vector.tensor_copy(skip[u % PACK], h[divmod(u, PACK)][:].indirect(pos2_sb[:]))
            nc.vector.tensor_tensor(logit[:, u, :], y[u][:], skip[u % PACK], ALU.mult)

        def sigmoid(u):
            nc.scalar.activation(result[:, u, :], logit[:, u, :], ACT.Sigmoid)

        def log_of(tiles, cols, bias):
            nc.scalar.activation(result[:, tiles, cols], result[:, tiles, cols], ACT.Ln, bias=bias)

        def finish(tiles, cols):
            b = tiles.start // PACK
            rows = out[b * PASS : (b + 1) * PASS, :].rearrange("(p t) m -> p t m", t=PACK)
            nc.vector.tensor_tensor(result[:, tiles, cols], result[:, tiles, cols], logit[:, tiles, cols], ALU.min)
            nc.sync.dma_start(rows[:, tiles.start - PACK * b : tiles.stop - PACK * b, cols], result[:, tiles, cols])

        first_tiles = slice(0, PACK)
        column_halves = (slice(0, NP // 2), slice(NP // 2, NP))
        for u in range(PACK):
            logits(u)
            sigmoid(u)
        for cols in column_halves:
            log_of(first_tiles, cols, floor[:])
        for u in range(PACK, TILES):
            logits(u)
        for cols in column_halves:
            finish(first_tiles, cols)
        for u in range(PACK, TILES):
            sigmoid(u)
        late_floor = skip[PACK - 1][:, 0:1]
        nc.gpsimd.memset(late_floor, LATE_FLOOR)
        for u in range(PACK, TILES):
            log_of(slice(u, u + 1), slice(0, NP), late_floor)
            finish(slice(u, u + 1), slice(0, NP))
